import numpy as np
import ml_dtypes


def mxq(x, axis, fmt="e4m3"):
    dtype, down = {"e4m3": (ml_dtypes.float8_e4m3fn, 7), "e5m2": (ml_dtypes.float8_e5m2, 14)}[fmt]
    v = np.moveaxis(np.asarray(x, np.float32).astype(ml_dtypes.bfloat16).astype(np.float64), axis, -1)
    blocks = v.reshape(v.shape[:-1] + (-1, 32))
    amax = np.abs(blocks).max(-1, keepdims=True)
    byte = np.maximum(np.where(amax > 0, np.frexp(amax)[1] - 1 + 127, 0) - down, 1)
    scale = np.exp2(byte - 127.0)
    codes = (blocks / scale).astype(np.float32).astype(dtype).astype(np.float64)
    return np.moveaxis((codes * scale).reshape(v.shape), -1, axis)


WIDE = False


def mx_kscale(k):
    if not WIDE:
        return np.ones(k)
    levels = np.array([24, -24, 12, -12, 0])
    if k % 512:
        return np.exp2(np.random.permutation(np.resize(levels, k // 32))).repeat(32)
    a = np.empty((k // 512, 16))
    for p in range(k // 512):
        a[p, :8] = np.random.permutation(np.resize(levels, 8))
        for g in range(8):
            far = levels[np.abs(levels - a[p, g]) >= 10]
            a[p, g + 8] = far[np.random.randint(len(far))]
    return np.exp2(a.ravel()).repeat(32)


def f64(x):
    return np.asarray(x).astype(np.float64)


def striped(idx):
    return np.tile(idx.reshape(-1, 16).T, (8, 1)).astype(np.uint16)


def unstriped(offs):
    return offs[:16].T.reshape(-1).astype(np.int64)


E2M1 = np.array([0.0, 0.5, 1.0, 1.5, 2.0, 3.0, 4.0, 6.0, -0.0, -0.5, -1.0, -1.5, -2.0, -3.0, -4.0, -6.0])


def pack_weight(w, fmt):
    k, n = w.shape
    w = f64(np.asarray(w, np.float32).astype(ml_dtypes.bfloat16)).reshape(k // 32, 32, n)
    amax = np.abs(w).max(1)
    if fmt == "e4m3":
        byte = np.frexp(amax)[1] - 1 + 127 - 7
    else:
        mant, ex = np.frexp(amax / 6.0)
        byte = np.where(mant > 0.5, ex, ex - 1) + 127
    byte = np.clip(np.where(amax > 0, byte, 1), 1, 254)
    scaled = (w * np.exp2(127.0 - byte)[:, None, :]).reshape(k, n).astype(np.float32)
    by_word = np.ascontiguousarray(scaled.reshape(k // 512, 128, 4, n).transpose(0, 1, 3, 2))
    if fmt == "e4m3":
        words = by_word.astype(ml_dtypes.float8_e4m3fn).view(np.uint8)
    else:
        c = by_word.astype(ml_dtypes.float4_e2m1fn).view(np.uint8) & 0xF
        words = (c[..., 0::2] | (c[..., 1::2] << 4)).reshape(k // 512, 128, 2 * n)
    return np.ascontiguousarray(words), np.ascontiguousarray(byte.astype(np.uint8).reshape(k // 512, 16, n))


def unpack_weight(words, scales, fmt):
    g, _, n = scales.shape
    words = np.ascontiguousarray(words).reshape(g, 128, n, -1)
    if fmt == "e4m3":
        vals = words.view(ml_dtypes.float8_e4m3fn).astype(np.float64)
    else:
        nib = np.empty((g, 128, n, 4), np.uint8)
        nib[..., 0::2] = words & 0xF
        nib[..., 1::2] = words >> 4
        vals = E2M1[nib]
    vals = vals * np.repeat(np.exp2(scales.astype(np.float64) - 127.0), 8, axis=1)[..., None]
    return vals.transpose(0, 1, 3, 2).reshape(g * 512, n)


K, L, N, T, J = 512, 1024, 512, 2048, 1024


def setup_inputs():
    n = np.random.standard_normal
    s = mx_kscale(K)[:, None]
    s2 = mx_kscale(L)[:, None]
    p_tab = pack_weight(n((K, T)) * s, "e4m3")
    p_wx = pack_weight(n((L, N)) / np.sqrt(L) / s2, "e4m3")
    return {
        "tab_words": p_tab[0],
        "tab_scales": p_tab[1],
        "wt": (n((K, N)) / np.sqrt(K) / s).astype(np.float32),
        "x": (n((L, J)) * s2).astype(np.float32),
        "wx_words": p_wx[0],
        "wx_scales": p_wx[1],
        "rT": (n((N, T))).astype(np.float32),
        "offs": striped(np.random.permutation(T)[:J]),
    }


def reference(tab_words, tab_scales, wt, x, wx_words, wx_scales, rT, offs):
    idx = unstriped(offs)
    tab_ = unpack_weight(tab_words, tab_scales, "e4m3")[:, idx]
    wt_q_ = mxq(f64(wt), 0, "e4m3")
    wt_r_ = mxq(f64(wt) - wt_q_, 0, "e4m3")
    x_ = mxq(f64(x), 0, "e4m3")
    wx_ = unpack_weight(wx_words, wx_scales, "e4m3")
    y = wt_q_.T @ tab_ + wt_r_.T @ tab_ + wx_.T @ x_
    return y + f64(rT)[:, idx]

@@ -1,0 +1,162 @@
+from contextlib import ExitStack
+
+import concourse.mybir as mybir
+from concourse.masks import make_identity
+
+K, L, N, T, J = 512, 1024, 512, 2048, 1024
+FLOPS = 2 * K * N * J * 2 + 2 * L * N * J + 2 * K * K * N
+
+F32 = mybir.dt.float32
+BF16 = mybir.dt.bfloat16
+I32 = mybir.dt.int32
+U32 = mybir.dt.uint32
+U16 = mybir.dt.uint16
+U8 = mybir.dt.uint8
+FP8X4 = mybir.dt.float8_e4m3fn_x4
+
+P = 128
+PACK = 4
+K_PASS = P * PACK
+BANK = 512
+N_BLOCKS = N // P
+J_HALVES = J // BANK
+X_PASSES = L // K_PASS
+RUN = 4
+
+
+def by_runs_src(ap):
+    return ap.rearrange("p t (c i) -> p c t i", i=RUN)
+
+
+def by_runs_dst(ap):
+    return ap.rearrange("p (c i) t -> p c t i", i=RUN)
+
+
+def quantize(nc, codes, scales, grouped):
+    nc.vector.quantize_mx(out=codes.bitcast(FP8X4), scales=scales, in_=grouped.rearrange("p w t -> p (w t)"))
+
+
+def mx(nc, out, lhs, lhs_scale, rhs, rhs_scale, start, stop):
+    nc.tensor.matmul_mx(out=out, lhsT=lhs.bitcast(FP8X4), lhsT_scale=lhs_scale,
+                        rhs=rhs.bitcast(FP8X4), rhs_scale=rhs_scale, start=start, stop=stop)
+
+
+def tile_list_tiert_resL_kernel(
+    tc, tab_words, tab_scales, wt, x, wx_words, wx_scales, rT, offs, out
+):
+    nc = tc.nc
+    with ExitStack() as ctx:
+        sb = ctx.enter_context(tc.tile_pool(name="sb", bufs=1))
+        psum = ctx.enter_context(tc.psum_pool(name="psum", bufs=1))
+
+        offsets = sb.tile([P, J // 16], U16, name="offsets")
+        tab_w = sb.tile([P, T], I32, name="tab_w", align_bytes=64)
+        tab_s = sb.tile([P, T], U8, name="tab_s", align_bytes=64)
+        wx_w = sb.tile([P, X_PASSES, N], I32, name="wx_w", align_bytes=64)
+        wx_s = sb.tile([P, X_PASSES, N], U8, name="wx_s", align_bytes=64)
+        wt_raw = sb.tile([P, PACK, N], F32, name="wt_raw", align_bytes=64)
+        x_raw = {}
+        for h in range(J_HALVES):
+            for a in range(X_PASSES):
+                x_raw[a, h] = sb.tile([P, PACK, BANK], F32, name="x_raw%d%d" % (a, h), align_bytes=64)
+        r_rows = [sb.tile([P, T], F32, name="r_rows%d" % b, align_bytes=64) for b in range(N_BLOCKS)]
+
+        nc.vector.memset(tab_s[:].bitcast(I32), 0)
+        nc.gpsimd.memset(wx_s[:].rearrange("p a n -> p (a n)").bitcast(I32), 0)
+
+        def load_x(a, h):
+            rows = x[a * K_PASS : (a + 1) * K_PASS, h * BANK : (h + 1) * BANK]
+            nc.sync.dma_start(out=x_raw[a, h][:], in_=rows.rearrange("(p t) j -> p t j", t=PACK))
+
+        nc.sync.dma_start(offsets[:], offs)
+        tab_src = tab_words[0].rearrange("p t i -> p (t i)").bitcast(I32)
+        for q in range(4):
+            nc.sync.dma_start(out=tab_w[:, q * BANK : (q + 1) * BANK], in_=tab_src[:, q * BANK : (q + 1) * BANK])
+        for q in range(4):
+            nc.sync.dma_start(out=tab_s[32 * q : 32 * q + 4, :].bitcast(I32),
+                              in_=tab_scales[0, 4 * q : 4 * q + 4, :].bitcast(I32))
+        nc.sync.dma_start(out=wt_raw[:], in_=wt.rearrange("(p t) n -> p t n", t=PACK))
+        load_x(0, 0)
+        load_x(1, 0)
+        nc.sync.dma_start(out=wx_w[:], in_=wx_words.rearrange("a p n i -> p a (n i)").bitcast(I32))
+        for q in range(4):
+            nc.sync.dma_start(out=wx_s[32 * q : 32 * q + 4, :, :].bitcast(I32),
+                              in_=wx_scales[:, 4 * q : 4 * q + 4, :].rearrange("a r n -> r a n").bitcast(I32))
+        load_x(0, 1)
+        load_x(1, 1)
+        for b in range(N_BLOCKS):
+            nc.sync.dma_start(out=r_rows[b][:], in_=rT[b * P : (b + 1) * P, :])
+
+        eye = sb.tile([P, P], BF16, name="eye", align_bytes=64)
+        make_identity(nc, eye[:])
+        eye_in = sb.tile([P, PACK * P, PACK], BF16, name="eye_in", align_bytes=64)
+        nc.vector.memset(eye_in[:], 0.0)
+        for t in range(PACK):
+            nc.vector.tensor_copy(out=eye_in[:, t * P : (t + 1) * P, t], in_=eye[:])
+        eye_c = sb.tile([P, PACK * P], U32, name="eye_c", align_bytes=64)
+        eye_s = sb.tile([P, PACK * P], U8, name="eye_s", align_bytes=64)
+        quantize(nc, eye_c[:], eye_s[:], eye_in[:])
+
+        v_c = sb.tile([P, J], U32, name="v_c", align_bytes=64)
+        v_s = sb.tile([P, J], U8, name="v_s", align_bytes=64)
+        nc.vector.tensor_copy(v_c[:], tab_w[:].bitcast(U32).indirect(offsets[:]))
+        nc.vector.tensor_copy(v_s[:], tab_s[:].indirect(offsets[:]))
+
+        wq_in = sb.tile([P, N, PACK], BF16, name="wq_in", align_bytes=64)
+        nc.scalar.copy(out=by_runs_dst(wq_in[:]), in_=by_runs_src(wt_raw[:]))
+        wq_c = sb.tile([P, N], U32, name="wq_c", align_bytes=64)
+        wq_s = sb.tile([P, N], U8, name="wq_s", align_bytes=64)
+        quantize(nc, wq_c[:], wq_s[:], wq_in[:])
+
+        wr_in = sb.tile([P, N, PACK], BF16, name="wr_in", align_bytes=64)
+        for b in range(N_BLOCKS):
+            cols = slice(b * P, (b + 1) * P)
+            decoded = psum.tile([P, PACK, P], F32, name="decoded%d" % b, tag="bank%d" % (N_BLOCKS + b))
+            for t in range(PACK):
+                rows = slice(t * P, (t + 1) * P)
+                mx(nc, decoded[:, t, :], eye_c[:, rows], eye_s[:, rows], wq_c[:, cols], wq_s[:, cols], True, True)
+            nc.vector.tensor_tensor(out=by_runs_dst(wr_in[:, cols, :]), in0=by_runs_src(wt_raw[:, :, cols]),
+                                    in1=by_runs_src(decoded[:]), op=mybir.AluOpType.subtract)
+        wr_c = sb.tile([P, N], U32, name="wr_c", align_bytes=64)
+        wr_s = sb.tile([P, N], U8, name="wr_s", align_bytes=64)
+        quantize(nc, wr_c[:], wr_s[:], wr_in[:])
+
+        x_c, x_s = {}, {}
+        for h in range(J_HALVES):
+            for a in range(X_PASSES):
+                x_in = sb.tile([P, BANK, PACK], BF16, name="x_in%d%d" % (a, h), align_bytes=64)
+                if (a, h) == (X_PASSES - 1, J_HALVES - 1):
+                    nc.vector.tensor_copy(out=by_runs_dst(x_in[:]), in_=by_runs_src(x_raw[a, h][:]))
+                else:
+                    nc.scalar.copy(out=by_runs_dst(x_in[:]), in_=by_runs_src(x_raw[a, h][:]))
+                x_c[a, h] = sb.tile([P, BANK], U32, name="x_c%d%d" % (a, h), align_bytes=64)
+                x_s[a, h] = sb.tile([P, BANK], U8, name="x_s%d%d" % (a, h), align_bytes=64)
+                quantize(nc, x_c[a, h][:], x_s[a, h][:], x_in[:])
+
+        y = {}
+        for h in range(J_HALVES):
+            toks = slice(h * BANK, (h + 1) * BANK)
+            acc = [psum.tile([P, BANK], F32, name="acc%d%d" % (b, h), tag="bank%d" % (N_BLOCKS * h + b))
+                   for b in range(N_BLOCKS)]
+            for b in range(N_BLOCKS):
+                cols = slice(b * P, (b + 1) * P)
+                mx(nc, acc[b][:], wq_c[:, cols], wq_s[:, cols], v_c[:, toks], v_s[:, toks], True, False)
+            for b in range(N_BLOCKS):
+                cols = slice(b * P, (b + 1) * P)
+                mx(nc, acc[b][:], wr_c[:, cols], wr_s[:, cols], v_c[:, toks], v_s[:, toks], False, False)
+            for a in range(X_PASSES):
+                for b in range(N_BLOCKS):
+                    cols = slice(b * P, (b + 1) * P)
+                    mx(nc, acc[b][:], wx_w[:, a, cols], wx_s[:, a, cols], x_c[a, h][:], x_s[a, h][:],
+                       False, a == X_PASSES - 1)
+            for b in range(N_BLOCKS):
+                y[b, h] = sb.tile([P, BANK], F32, name="y%d%d" % (b, h), align_bytes=64)
+                nc.scalar.copy(out=y[b, h][:], in_=acc[b][:])
+
+        per_half = BANK // 16
+        for b in range(N_BLOCKS):
+            for h in range(J_HALVES):
+                res = sb.tile([P, BANK], F32, name="res%d%d" % (b, h), align_bytes=64)
+                picked = r_rows[b][:].indirect(offsets[:, h * per_half : (h + 1) * per_half])
+                nc.vector.tensor_tensor(res[:], picked, y[b, h][:], mybir.AluOpType.add)
+                nc.sync.dma_start(out=out[b * P : (b + 1) * P, h * BANK : (h + 1) * BANK], in_=res[:])

@@ -55,60 +55,63 @@ def tile_list_tiert_resL_kernel(
         wx_w = sb.tile([P, X_PASSES, N], I32, name="wx_w", align_bytes=64)
         wx_s = sb.tile([P, X_PASSES, N], U8, name="wx_s", align_bytes=64)
         wt_raw = sb.tile([P, PACK, N], F32, name="wt_raw", align_bytes=64)
+        x_first = sb.tile([P, PACK, J], F32, name="x_first", tag="x_first", align_bytes=64)
+        x_last = [sb.tile([P, PACK, BANK], F32, name="x_last%d" % h, align_bytes=64) for h in range(J_HALVES)]
         x_raw = {}
         for h in range(J_HALVES):
-            for a in range(X_PASSES):
-                x_raw[a, h] = sb.tile([P, PACK, BANK], F32, name="x_raw%d%d" % (a, h), align_bytes=64)
+            x_raw[0, h] = x_first[:, :, h * BANK : (h + 1) * BANK]
+            x_raw[1, h] = x_last[h][:]
         r_rows = [sb.tile([P, T], F32, name="r_rows%d" % b, align_bytes=64) for b in range(N_BLOCKS)]
 
         nc.vector.memset(tab_s[:].bitcast(I32), 0)
+        eye = sb.tile([P, P], BF16, name="eye", tag="first_stage", align_bytes=64)
+        eye_hi = sb.tile([P, 2 * P, PACK], BF16, name="eye_hi", tag="identity", align_bytes=64)
+        nc.gpsimd.memset(eye_hi[:].rearrange("p w t -> p (w t)").bitcast(I32), 0)
+        make_identity(nc, eye[:])
         nc.gpsimd.memset(wx_s[:].rearrange("p a n -> p (a n)").bitcast(I32), 0)
 
-        def load_x(a, h):
-            rows = x[a * K_PASS : (a + 1) * K_PASS, h * BANK : (h + 1) * BANK]
-            nc.sync.dma_start(out=x_raw[a, h][:], in_=rows.rearrange("(p t) j -> p t j", t=PACK))
-
         nc.sync.dma_start(offsets[:], offs)
-        tab_src = tab_words[0].rearrange("p t i -> p (t i)").bitcast(I32)
-        for q in range(4):
-            nc.sync.dma_start(out=tab_w[:, q * BANK : (q + 1) * BANK], in_=tab_src[:, q * BANK : (q + 1) * BANK])
+        wt_rows = wt.rearrange("(p t) n -> p t n", t=PACK)
+        for u in range(2):
+            nc.sync.dma_start(out=wt_raw[:, 2 * u : 2 * u + 2, :], in_=wt_rows[:, 2 * u : 2 * u + 2, :])
         for q in range(4):
             nc.sync.dma_start(out=tab_s[32 * q : 32 * q + 4, :].bitcast(I32),
                               in_=tab_scales[0, 4 * q : 4 * q + 4, :].bitcast(I32))
-        nc.sync.dma_start(out=wt_raw[:], in_=wt.rearrange("(p t) n -> p t n", t=PACK))
-        load_x(0, 0)
-        load_x(1, 0)
+        nc.sync.dma_start(out=tab_w[:], in_=tab_words[0].rearrange("p t i -> p (t i)").bitcast(I32))
+        x_rows = x.rearrange("(a p t) j -> a p t j", p=P, t=PACK)
+        nc.sync.dma_start(out=x_first[:], in_=x_rows[0])
         nc.sync.dma_start(out=wx_w[:], in_=wx_words.rearrange("a p n i -> p a (n i)").bitcast(I32))
         for q in range(4):
             nc.sync.dma_start(out=wx_s[32 * q : 32 * q + 4, :, :].bitcast(I32),
                               in_=wx_scales[:, 4 * q : 4 * q + 4, :].rearrange("a r n -> r a n").bitcast(I32))
-        load_x(0, 1)
-        load_x(1, 1)
+        for h in range(J_HALVES):
+            nc.sync.dma_start(out=x_last[h][:], in_=x_rows[1, :, :, h * BANK : (h + 1) * BANK])
         for b in range(N_BLOCKS):
             nc.sync.dma_start(out=r_rows[b][:], in_=rT[b * P : (b + 1) * P, :])
 
-        eye = sb.tile([P, P], BF16, name="eye", align_bytes=64)
-        make_identity(nc, eye[:])
-        eye_in = sb.tile([P, PACK * P, PACK], BF16, name="eye_in", align_bytes=64)
-        nc.vector.memset(eye_in[:], 0.0)
-        for t in range(PACK):
-            nc.vector.tensor_copy(out=eye_in[:, t * P : (t + 1) * P, t], in_=eye[:])
         eye_c = sb.tile([P, PACK * P], U32, name="eye_c", align_bytes=64)
         eye_s = sb.tile([P, PACK * P], U8, name="eye_s", align_bytes=64)
-        quantize(nc, eye_c[:], eye_s[:], eye_in[:])
+        eye_lo = sb.tile([P, 2 * P, PACK], BF16, name="eye_lo", align_bytes=64)
+        nc.vector.memset(eye_lo[:], 0.0)
+        for t in range(2):
+            nc.vector.tensor_copy(out=eye_lo[:, t * P : (t + 1) * P, t], in_=eye[:])
+            nc.scalar.copy(out=eye_hi[:, t * P : (t + 1) * P, 2 + t], in_=eye[:])
+        quantize(nc, eye_c[:, : 2 * P], eye_s[:, : 2 * P], eye_lo[:])
+        quantize(nc, eye_c[:, 2 * P :], eye_s[:, 2 * P :], eye_hi[:])
 
-        v_c = sb.tile([P, J], U32, name="v_c", align_bytes=64)
-        v_s = sb.tile([P, J], U8, name="v_s", align_bytes=64)
-        nc.vector.tensor_copy(v_c[:], tab_w[:].bitcast(U32).indirect(offsets[:]))
+        v_s = sb.tile([P, J], U8, name="v_s", tag="identity", align_bytes=64)
         nc.vector.tensor_copy(v_s[:], tab_s[:].indirect(offsets[:]))
 
-        wq_in = sb.tile([P, N, PACK], BF16, name="wq_in", align_bytes=64)
+        wq_in = sb.tile([P, N, PACK], BF16, name="wq_in", tag="first_stage", align_bytes=64)
         nc.scalar.copy(out=by_runs_dst(wq_in[:]), in_=by_runs_src(wt_raw[:]))
         wq_c = sb.tile([P, N], U32, name="wq_c", align_bytes=64)
         wq_s = sb.tile([P, N], U8, name="wq_s", align_bytes=64)
         quantize(nc, wq_c[:], wq_s[:], wq_in[:])
 
-        wr_in = sb.tile([P, N, PACK], BF16, name="wr_in", align_bytes=64)
+        v_c = sb.tile([P, J], U32, name="v_c", tag="first_stage", align_bytes=64)
+        nc.vector.tensor_copy(v_c[:], tab_w[:].bitcast(U32).indirect(offsets[:]))
+
+        wr_in = sb.tile([P, N, PACK], BF16, name="wr_in", tag="vector_stage", align_bytes=64)
         for b in range(N_BLOCKS):
             cols = slice(b * P, (b + 1) * P)
             decoded = psum.tile([P, PACK, P], F32, name="decoded%d" % b, tag="bank%d" % (N_BLOCKS + b))
@@ -122,41 +125,55 @@ def tile_list_tiert_resL_kernel(
         quantize(nc, wr_c[:], wr_s[:], wr_in[:])
 
         x_c, x_s = {}, {}
-        for h in range(J_HALVES):
-            for a in range(X_PASSES):
-                x_in = sb.tile([P, BANK, PACK], BF16, name="x_in%d%d" % (a, h), align_bytes=64)
-                if (a, h) == (X_PASSES - 1, J_HALVES - 1):
-                    nc.vector.tensor_copy(out=by_runs_dst(x_in[:]), in_=by_runs_src(x_raw[a, h][:]))
-                else:
-                    nc.scalar.copy(out=by_runs_dst(x_in[:]), in_=by_runs_src(x_raw[a, h][:]))
-                x_c[a, h] = sb.tile([P, BANK], U32, name="x_c%d%d" % (a, h), align_bytes=64)
-                x_s[a, h] = sb.tile([P, BANK], U8, name="x_s%d%d" % (a, h), align_bytes=64)
-                quantize(nc, x_c[a, h][:], x_s[a, h][:], x_in[:])
+        stage_tag = {(0, 0): "x_in00", (0, 1): "vector_stage", (1, 0): "last_stage", (1, 1): "last_stage"}
+        x_in = {}
 
-        y = {}
+        def interleave_x(a, h):
+            x_in[a, h] = sb.tile([P, BANK, PACK], BF16, name="x_in%d%d" % (a, h), tag=stage_tag[a, h], align_bytes=64)
+            if h == 1:
+                nc.vector.tensor_copy(out=by_runs_dst(x_in[a, h][:]), in_=by_runs_src(x_raw[a, h]))
+            else:
+                nc.scalar.copy(out=by_runs_dst(x_in[a, h][:]), in_=by_runs_src(x_raw[a, h]))
+
+        def quantize_x(a, h):
+            x_c[a, h] = sb.tile([P, BANK], U32, name="x_c%d%d" % (a, h),
+                                tag="x_first" if (a, h) == (0, 0) else "x_c%d%d" % (a, h), align_bytes=64)
+            x_s[a, h] = sb.tile([P, BANK], U8, name="x_s%d%d" % (a, h), align_bytes=64)
+            quantize(nc, x_c[a, h][:], x_s[a, h][:], x_in[a, h][:])
+
+        interleave_x(0, 0)
+        interleave_x(0, 1)
+        quantize_x(0, 0)
+        quantize_x(0, 1)
+        for h in range(J_HALVES):
+            interleave_x(1, h)
+            quantize_x(1, h)
+
+        banks = [(b, h) for h in range(J_HALVES) for b in range(N_BLOCKS)]
+        acc = {}
+        for b, h in banks:
+            acc[b, h] = psum.tile([P, BANK], F32, name="acc%d%d" % (b, h), tag="bank%d" % (N_BLOCKS * h + b))
         for h in range(J_HALVES):
             toks = slice(h * BANK, (h + 1) * BANK)
-            acc = [psum.tile([P, BANK], F32, name="acc%d%d" % (b, h), tag="bank%d" % (N_BLOCKS * h + b))
-                   for b in range(N_BLOCKS)]
-            for b in range(N_BLOCKS):
-                cols = slice(b * P, (b + 1) * P)
-                mx(nc, acc[b][:], wq_c[:, cols], wq_s[:, cols], v_c[:, toks], v_s[:, toks], True, False)
-            for b in range(N_BLOCKS):
-                cols = slice(b * P, (b + 1) * P)
-                mx(nc, acc[b][:], wr_c[:, cols], wr_s[:, cols], v_c[:, toks], v_s[:, toks], False, False)
+            for first, w_c, w_s in ((True, wq_c, wq_s), (False, wr_c, wr_s)):
+                for b in range(N_BLOCKS):
+                    cols = slice(b * P, (b + 1) * P)
+                    mx(nc, acc[b, h][:], w_c[:, cols], w_s[:, cols], v_c[:, toks], v_s[:, toks], first, False)
             for a in range(X_PASSES):
                 for b in range(N_BLOCKS):
                     cols = slice(b * P, (b + 1) * P)
-                    mx(nc, acc[b][:], wx_w[:, a, cols], wx_s[:, a, cols], x_c[a, h][:], x_s[a, h][:],
+                    mx(nc, acc[b, h][:], wx_w[:, a, cols], wx_s[:, a, cols], x_c[a, h][:], x_s[a, h][:],
                        False, a == X_PASSES - 1)
-            for b in range(N_BLOCKS):
-                y[b, h] = sb.tile([P, BANK], F32, name="y%d%d" % (b, h), align_bytes=64)
-                nc.scalar.copy(out=y[b, h][:], in_=acc[b][:])
-
         per_half = BANK // 16
         for b in range(N_BLOCKS):
+            res = sb.tile([P, J], F32, name="res%d" % b, align_bytes=64)
             for h in range(J_HALVES):
-                res = sb.tile([P, BANK], F32, name="res%d%d" % (b, h), align_bytes=64)
+                toks = slice(h * BANK, (h + 1) * BANK)
+                y = sb.tile([P, BANK], F32, name="y%d%d" % (b, h), align_bytes=64)
+                nc.scalar.copy(out=y[:], in_=acc[b, h][:])
                 picked = r_rows[b][:].indirect(offsets[:, h * per_half : (h + 1) * per_half])
-                nc.vector.tensor_tensor(res[:], picked, y[b, h][:], mybir.AluOpType.add)
-                nc.sync.dma_start(out=out[b * P : (b + 1) * P, h * BANK : (h + 1) * BANK], in_=res[:])
+                nc.vector.tensor_tensor(res[:, toks], picked, y[:], mybir.AluOpType.add)
+                if b == N_BLOCKS - 1:
+                    nc.sync.dma_start(out=out[b * P : (b + 1) * P, toks], in_=res[:, toks])
+            if b < N_BLOCKS - 1:
+                nc.sync.dma_start(out=out[b * P : (b + 1) * P, :], in_=res[:])

@@ -64,11 +64,11 @@ def tile_list_tiert_resL_kernel(
         r_rows = [sb.tile([P, T], F32, name="r_rows%d" % b, align_bytes=64) for b in range(N_BLOCKS)]
 
         nc.vector.memset(tab_s[:].bitcast(I32), 0)
+        nc.vector.memset(wx_s[:].rearrange("p a n -> p (a n)").bitcast(I32), 0)
         eye = sb.tile([P, P], BF16, name="eye", tag="first_stage", align_bytes=64)
         eye_hi = sb.tile([P, 2 * P, PACK], BF16, name="eye_hi", tag="identity", align_bytes=64)
         nc.gpsimd.memset(eye_hi[:].rearrange("p w t -> p (w t)").bitcast(I32), 0)
         make_identity(nc, eye[:])
-        nc.gpsimd.memset(wx_s[:].rearrange("p a n -> p (a n)").bitcast(I32), 0)
 
         nc.sync.dma_start(offsets[:], offs)
         wt_rows = wt.rearrange("(p t) n -> p t n", t=PACK)
@@ -80,12 +80,12 @@ def tile_list_tiert_resL_kernel(
         nc.sync.dma_start(out=tab_w[:], in_=tab_words[0].rearrange("p t i -> p (t i)").bitcast(I32))
         x_rows = x.rearrange("(a p t) j -> a p t j", p=P, t=PACK)
         nc.sync.dma_start(out=x_first[:], in_=x_rows[0])
-        nc.sync.dma_start(out=wx_w[:], in_=wx_words.rearrange("a p n i -> p a (n i)").bitcast(I32))
+        for h in range(J_HALVES):
+            nc.sync.dma_start(out=x_last[h][:], in_=x_rows[1, :, :, h * BANK : (h + 1) * BANK])
         for q in range(4):
             nc.sync.dma_start(out=wx_s[32 * q : 32 * q + 4, :, :].bitcast(I32),
                               in_=wx_scales[:, 4 * q : 4 * q + 4, :].rearrange("a r n -> r a n").bitcast(I32))
-        for h in range(J_HALVES):
-            nc.sync.dma_start(out=x_last[h][:], in_=x_rows[1, :, :, h * BANK : (h + 1) * BANK])
+        nc.sync.dma_start(out=wx_w[:], in_=wx_words.rearrange("a p n i -> p a (n i)").bitcast(I32))
         for b in range(N_BLOCKS):
             nc.sync.dma_start(out=r_rows[b][:], in_=rT[b * P : (b + 1) * P, :])
 
@@ -125,55 +125,52 @@ def tile_list_tiert_resL_kernel(
         quantize(nc, wr_c[:], wr_s[:], wr_in[:])
 
         x_c, x_s = {}, {}
-        stage_tag = {(0, 0): "x_in00", (0, 1): "vector_stage", (1, 0): "last_stage", (1, 1): "last_stage"}
-        x_in = {}
+        for a in range(X_PASSES):
+            for h in range(J_HALVES):
+                x_s[a, h] = sb.tile([P, BANK], U8, name="x_s%d%d" % (a, h), align_bytes=64)
 
-        def interleave_x(a, h):
-            x_in[a, h] = sb.tile([P, BANK, PACK], BF16, name="x_in%d%d" % (a, h), tag=stage_tag[a, h], align_bytes=64)
-            if h == 1:
-                nc.vector.tensor_copy(out=by_runs_dst(x_in[a, h][:]), in_=by_runs_src(x_raw[a, h]))
-            else:
-                nc.scalar.copy(out=by_runs_dst(x_in[a, h][:]), in_=by_runs_src(x_raw[a, h]))
+        def interleave(copy, src, tag):
+            staged = sb.tile([P, src.shape[2], PACK], BF16, name="staged_" + tag, tag=tag, align_bytes=64)
+            copy(out=by_runs_dst(staged[:]), in_=by_runs_src(src))
+            return staged
 
-        def quantize_x(a, h):
-            x_c[a, h] = sb.tile([P, BANK], U32, name="x_c%d%d" % (a, h),
-                                tag="x_first" if (a, h) == (0, 0) else "x_c%d%d" % (a, h), align_bytes=64)
-            x_s[a, h] = sb.tile([P, BANK], U8, name="x_s%d%d" % (a, h), align_bytes=64)
-            quantize(nc, x_c[a, h][:], x_s[a, h][:], x_in[a, h][:])
+        staged_00 = interleave(nc.scalar.copy, x_raw[0, 0], "x_in00")
+        staged_01 = interleave(nc.vector.tensor_copy, x_raw[0, 1], "vector_stage")
+        x_c[0, 0] = sb.tile([P, BANK], U32, name="x_c00", tag="x_first", align_bytes=64)
+        x_c[0, 1] = sb.tile([P, BANK], U32, name="x_c01", align_bytes=64)
+        quantize(nc, x_c[0, 0][:], x_s[0, 0][:], staged_00[:])
+        quantize(nc, x_c[0, 1][:], x_s[0, 1][:], staged_01[:])
 
-        interleave_x(0, 0)
-        interleave_x(0, 1)
-        quantize_x(0, 0)
-        quantize_x(0, 1)
-        for h in range(J_HALVES):
-            interleave_x(1, h)
-            quantize_x(1, h)
+        x_c[1, 0] = sb.tile([P, BANK], U32, name="x_c10", align_bytes=64)
+        x_c[1, 1] = sb.tile([P, BANK], U32, name="x_c11", align_bytes=64)
+        staged_10 = interleave(nc.scalar.copy, x_raw[1, 0], "last_stage")
+        quantize(nc, x_c[1, 0][:], x_s[1, 0][:], staged_10[:])
+        lo, hi = slice(0, BANK // 2), slice(BANK // 2, BANK)
+        staged_lo = interleave(nc.vector.tensor_copy, x_raw[1, 1][:, :, lo], "last_stage")
+        staged_hi = interleave(nc.scalar.copy, x_raw[1, 1][:, :, hi], "x_in11")
+        quantize(nc, x_c[1, 1][:, lo], x_s[1, 1][:, lo], staged_lo[:])
+        quantize(nc, x_c[1, 1][:, hi], x_s[1, 1][:, hi], staged_hi[:])
 
-        banks = [(b, h) for h in range(J_HALVES) for b in range(N_BLOCKS)]
-        acc = {}
-        for b, h in banks:
-            acc[b, h] = psum.tile([P, BANK], F32, name="acc%d%d" % (b, h), tag="bank%d" % (N_BLOCKS * h + b))
-        for h in range(J_HALVES):
-            toks = slice(h * BANK, (h + 1) * BANK)
-            for first, w_c, w_s in ((True, wq_c, wq_s), (False, wr_c, wr_s)):
-                for b in range(N_BLOCKS):
-                    cols = slice(b * P, (b + 1) * P)
-                    mx(nc, acc[b, h][:], w_c[:, cols], w_s[:, cols], v_c[:, toks], v_s[:, toks], first, False)
-            for a in range(X_PASSES):
-                for b in range(N_BLOCKS):
-                    cols = slice(b * P, (b + 1) * P)
-                    mx(nc, acc[b, h][:], wx_w[:, a, cols], wx_s[:, a, cols], x_c[a, h][:], x_s[a, h][:],
-                       False, a == X_PASSES - 1)
-        per_half = BANK // 16
         for b in range(N_BLOCKS):
+            cols = slice(b * P, (b + 1) * P)
             res = sb.tile([P, J], F32, name="res%d" % b, align_bytes=64)
             for h in range(J_HALVES):
                 toks = slice(h * BANK, (h + 1) * BANK)
+                acc = psum.tile([P, BANK], F32, name="acc%d%d" % (b, h), tag="bank%d" % (N_BLOCKS * h + b))
+                mx(nc, acc[:], wq_c[:, cols], wq_s[:, cols], v_c[:, toks], v_s[:, toks], True, False)
+                mx(nc, acc[:], wr_c[:, cols], wr_s[:, cols], v_c[:, toks], v_s[:, toks], False, False)
+                for a in reversed(range(X_PASSES)):
+                    mx(nc, acc[:], wx_w[:, a, cols], wx_s[:, a, cols], x_c[a, h][:], x_s[a, h][:],
+                       False, a == 0)
                 y = sb.tile([P, BANK], F32, name="y%d%d" % (b, h), align_bytes=64)
-                nc.scalar.copy(out=y[:], in_=acc[b, h][:])
-                picked = r_rows[b][:].indirect(offsets[:, h * per_half : (h + 1) * per_half])
-                nc.vector.tensor_tensor(res[:, toks], picked, y[:], mybir.AluOpType.add)
-                if b == N_BLOCKS - 1:
-                    nc.sync.dma_start(out=out[b * P : (b + 1) * P, toks], in_=res[:, toks])
+                nc.scalar.copy(out=y[:], in_=acc[:])
+                last = (b, h) == (N_BLOCKS - 1, J_HALVES - 1)
+                width = BANK // 2 if last else BANK
+                for j0 in range(0, BANK, width):
+                    part = slice(h * BANK + j0, h * BANK + j0 + width)
+                    picked = r_rows[b][:].indirect(offsets[:, part.start // 16 : part.stop // 16])
+                    nc.vector.tensor_tensor(res[:, part], picked, y[:, j0 : j0 + width], mybir.AluOpType.add)
+                    if b == N_BLOCKS - 1:
+                        nc.sync.dma_start(out=out[cols, part], in_=res[:, part])
             if b < N_BLOCKS - 1:
-                nc.sync.dma_start(out=out[b * P : (b + 1) * P, :], in_=res[:])
+                nc.sync.dma_start(out=out[cols, :], in_=res[:])

@@ -52,15 +52,13 @@ def tile_list_tiert_resL_kernel(
         offsets = sb.tile([P, J // 16], U16, name="offsets")
         tab_w = sb.tile([P, T], I32, name="tab_w", align_bytes=64)
         tab_s = sb.tile([P, T], U8, name="tab_s", align_bytes=64)
-        wx_w = sb.tile([P, X_PASSES, N], I32, name="wx_w", align_bytes=64)
+        wx_w = [sb.tile([P, X_PASSES, N // 2], I32, name="wx_w%d" % g, align_bytes=64) for g in range(2)]
         wx_s = sb.tile([P, X_PASSES, N], U8, name="wx_s", align_bytes=64)
         wt_raw = sb.tile([P, PACK, N], F32, name="wt_raw", align_bytes=64)
-        x_first = sb.tile([P, PACK, J], F32, name="x_first", tag="x_first", align_bytes=64)
-        x_last = [sb.tile([P, PACK, BANK], F32, name="x_last%d" % h, align_bytes=64) for h in range(J_HALVES)]
         x_raw = {}
-        for h in range(J_HALVES):
-            x_raw[0, h] = x_first[:, :, h * BANK : (h + 1) * BANK]
-            x_raw[1, h] = x_last[h][:]
+        for a in range(X_PASSES):
+            for h in range(J_HALVES):
+                x_raw[a, h] = sb.tile([P, PACK, BANK], F32, name="x_raw%d%d" % (a, h), align_bytes=64)
         r_rows = [sb.tile([P, T], F32, name="r_rows%d" % b, align_bytes=64) for b in range(N_BLOCKS)]
 
         nc.vector.memset(tab_s[:].bitcast(I32), 0)
@@ -79,14 +77,16 @@ def tile_list_tiert_resL_kernel(
                               in_=tab_scales[0, 4 * q : 4 * q + 4, :].bitcast(I32))
         nc.sync.dma_start(out=tab_w[:], in_=tab_words[0].rearrange("p t i -> p (t i)").bitcast(I32))
         x_rows = x.rearrange("(a p t) j -> a p t j", p=P, t=PACK)
-        nc.sync.dma_start(out=x_first[:], in_=x_rows[0])
-        for h in range(J_HALVES):
-            nc.sync.dma_start(out=x_last[h][:], in_=x_rows[1, :, :, h * BANK : (h + 1) * BANK])
+        for a in range(X_PASSES):
+            for h in range(J_HALVES):
+                nc.sync.dma_start(out=x_raw[a, h][:], in_=x_rows[a, :, :, h * BANK : (h + 1) * BANK])
         for q in range(4):
             nc.sync.dma_start(out=wx_s[32 * q : 32 * q + 4, :, :].bitcast(I32),
                               in_=wx_scales[:, 4 * q : 4 * q + 4, :].rearrange("a r n -> r a n").bitcast(I32))
-        nc.sync.dma_start(out=wx_w[:], in_=wx_words.rearrange("a p n i -> p a (n i)").bitcast(I32))
+        wx_src = wx_words.rearrange("a p n i -> p a (n i)").bitcast(I32)
         for b in range(N_BLOCKS):
+            if b % 2 == 0:
+                nc.sync.dma_start(out=wx_w[b // 2][:], in_=wx_src[:, :, b * P : (b + 2) * P])
             nc.sync.dma_start(out=r_rows[b][:], in_=rT[b * P : (b + 1) * P, :])
 
         eye_c = sb.tile([P, PACK * P], U32, name="eye_c", align_bytes=64)
@@ -134,16 +134,16 @@ def tile_list_tiert_resL_kernel(
             copy(out=by_runs_dst(staged[:]), in_=by_runs_src(src))
             return staged
 
-        staged_00 = interleave(nc.scalar.copy, x_raw[0, 0], "x_in00")
-        staged_01 = interleave(nc.vector.tensor_copy, x_raw[0, 1], "vector_stage")
-        x_c[0, 0] = sb.tile([P, BANK], U32, name="x_c00", tag="x_first", align_bytes=64)
-        x_c[0, 1] = sb.tile([P, BANK], U32, name="x_c01", align_bytes=64)
+        staged_00 = interleave(nc.scalar.copy, x_raw[0, 0][:], "x_in00")
+        staged_01 = interleave(nc.scalar.copy, x_raw[0, 1][:], "x_in01")
+        x_c[0, 0] = sb.tile([P, BANK], U32, name="x_c00", tag="vector_stage", align_bytes=64)
         quantize(nc, x_c[0, 0][:], x_s[0, 0][:], staged_00[:])
+        x_c[0, 1] = sb.tile([P, BANK], U32, name="x_c01", tag="x_in00", align_bytes=64)
         quantize(nc, x_c[0, 1][:], x_s[0, 1][:], staged_01[:])
 
         x_c[1, 0] = sb.tile([P, BANK], U32, name="x_c10", align_bytes=64)
         x_c[1, 1] = sb.tile([P, BANK], U32, name="x_c11", align_bytes=64)
-        staged_10 = interleave(nc.scalar.copy, x_raw[1, 0], "last_stage")
+        staged_10 = interleave(nc.scalar.copy, x_raw[1, 0][:], "last_stage")
         quantize(nc, x_c[1, 0][:], x_s[1, 0][:], staged_10[:])
         lo, hi = slice(0, BANK // 2), slice(BANK // 2, BANK)
         staged_lo = interleave(nc.vector.tensor_copy, x_raw[1, 1][:, :, lo], "last_stage")
@@ -156,11 +156,11 @@ def tile_list_tiert_resL_kernel(
             res = sb.tile([P, J], F32, name="res%d" % b, align_bytes=64)
             for h in range(J_HALVES):
                 toks = slice(h * BANK, (h + 1) * BANK)
-                acc = psum.tile([P, BANK], F32, name="acc%d%d" % (b, h), tag="bank%d" % (N_BLOCKS * h + b))
+                acc = psum.tile([P, BANK], F32, name="acc%d%d" % (b, h), tag="bank%d" % (N_BLOCKS + b if h else b % 2))
                 mx(nc, acc[:], wq_c[:, cols], wq_s[:, cols], v_c[:, toks], v_s[:, toks], True, False)
                 mx(nc, acc[:], wr_c[:, cols], wr_s[:, cols], v_c[:, toks], v_s[:, toks], False, False)
                 for a in reversed(range(X_PASSES)):
-                    mx(nc, acc[:], wx_w[:, a, cols], wx_s[:, a, cols], x_c[a, h][:], x_s[a, h][:],
+                    mx(nc, acc[:], wx_w[b // 2][:, a, (b % 2) * P : (b % 2 + 1) * P], wx_s[:, a, cols], x_c[a, h][:], x_s[a, h][:],
                        False, a == 0)
                 y = sb.tile([P, BANK], F32, name="y%d%d" % (b, h), align_bytes=64)
                 nc.scalar.copy(out=y[:], in_=acc[:])

from contextlib import ExitStack

import concourse.mybir as mybir
from concourse.masks import make_identity

K, L, N, T, J = 512, 1024, 512, 2048, 1024
FLOPS = 2 * K * N * J * 2 + 2 * L * N * J + 2 * K * K * N

F32 = mybir.dt.float32
BF16 = mybir.dt.bfloat16
I32 = mybir.dt.int32
U32 = mybir.dt.uint32
U16 = mybir.dt.uint16
U8 = mybir.dt.uint8
FP8X4 = mybir.dt.float8_e4m3fn_x4

P = 128
PACK = 4
K_PASS = P * PACK
BANK = 512
N_BLOCKS = N // P
J_HALVES = J // BANK
X_PASSES = L // K_PASS
RUN = 4


def by_runs_src(ap):
    return ap.rearrange("p t (c i) -> p c t i", i=RUN)


def by_runs_dst(ap):
    return ap.rearrange("p (c i) t -> p c t i", i=RUN)


def quantize(nc, codes, scales, grouped):
    nc.vector.quantize_mx(out=codes.bitcast(FP8X4), scales=scales, in_=grouped.rearrange("p w t -> p (w t)"))


def mx(nc, out, lhs, lhs_scale, rhs, rhs_scale, start, stop):
    nc.tensor.matmul_mx(out=out, lhsT=lhs.bitcast(FP8X4), lhsT_scale=lhs_scale,
                        rhs=rhs.bitcast(FP8X4), rhs_scale=rhs_scale, start=start, stop=stop)


def tile_list_tiert_resL_kernel(
    tc, tab_words, tab_scales, wt, x, wx_words, wx_scales, rT, offs, out
):
    nc = tc.nc
    with ExitStack() as ctx:
        sb = ctx.enter_context(tc.tile_pool(name="sb", bufs=1))
        psum = ctx.enter_context(tc.psum_pool(name="psum", bufs=1))

        offsets = sb.tile([P, J // 16], U16, name="offsets")
        tab_w = sb.tile([P, T], I32, name="tab_w", align_bytes=64)
        tab_s = sb.tile([P, T], U8, name="tab_s", align_bytes=64)
        wx_w = [sb.tile([P, X_PASSES, N // 2], I32, name="wx_w%d" % g, align_bytes=64) for g in range(2)]
        wx_s = sb.tile([P, X_PASSES, N], U8, name="wx_s", align_bytes=64)
        wt_raw = sb.tile([P, PACK, N], F32, name="wt_raw", align_bytes=64)
        x_raw = {}
        for a in range(X_PASSES):
            for h in range(J_HALVES):
                x_raw[a, h] = sb.tile([P, PACK, BANK], F32, name="x_raw%d%d" % (a, h), align_bytes=64)
        r_rows = [sb.tile([P, T], F32, name="r_rows%d" % b, align_bytes=64) for b in range(N_BLOCKS)]

        nc.vector.memset(tab_s[:].bitcast(I32), 0)
        nc.vector.memset(wx_s[:].rearrange("p a n -> p (a n)").bitcast(I32), 0)
        eye = sb.tile([P, P], BF16, name="eye", tag="first_stage", align_bytes=64)
        eye_hi = sb.tile([P, 2 * P, PACK], BF16, name="eye_hi", tag="identity", align_bytes=64)
        nc.gpsimd.memset(eye_hi[:].rearrange("p w t -> p (w t)").bitcast(I32), 0)
        make_identity(nc, eye[:])

        nc.sync.dma_start(offsets[:], offs)
        wt_rows = wt.rearrange("(p t) n -> p t n", t=PACK)
        for u in range(2):
            nc.sync.dma_start(out=wt_raw[:, 2 * u : 2 * u + 2, :], in_=wt_rows[:, 2 * u : 2 * u + 2, :])
        for q in range(4):
            nc.sync.dma_start(out=tab_s[32 * q : 32 * q + 4, :].bitcast(I32),
                              in_=tab_scales[0, 4 * q : 4 * q + 4, :].bitcast(I32))
        nc.sync.dma_start(out=tab_w[:], in_=tab_words[0].rearrange("p t i -> p (t i)").bitcast(I32))
        x_rows = x.rearrange("(a p t) j -> a p t j", p=P, t=PACK)
        for a in range(X_PASSES):
            for h in range(J_HALVES):
                nc.sync.dma_start(out=x_raw[a, h][:], in_=x_rows[a, :, :, h * BANK : (h + 1) * BANK])
        for q in range(4):
            nc.sync.dma_start(out=wx_s[32 * q : 32 * q + 4, :, :].bitcast(I32),
                              in_=wx_scales[:, 4 * q : 4 * q + 4, :].rearrange("a r n -> r a n").bitcast(I32))
        wx_src = wx_words.rearrange("a p n i -> p a (n i)").bitcast(I32)
        for b in range(N_BLOCKS):
            if b % 2 == 0:
                nc.sync.dma_start(out=wx_w[b // 2][:], in_=wx_src[:, :, b * P : (b + 2) * P])
            nc.sync.dma_start(out=r_rows[b][:], in_=rT[b * P : (b + 1) * P, :])

        eye_c = sb.tile([P, PACK * P], U32, name="eye_c", align_bytes=64)
        eye_s = sb.tile([P, PACK * P], U8, name="eye_s", align_bytes=64)
        eye_lo = sb.tile([P, 2 * P, PACK], BF16, name="eye_lo", align_bytes=64)
        nc.vector.memset(eye_lo[:], 0.0)
        for t in range(2):
            nc.vector.tensor_copy(out=eye_lo[:, t * P : (t + 1) * P, t], in_=eye[:])
            nc.scalar.copy(out=eye_hi[:, t * P : (t + 1) * P, 2 + t], in_=eye[:])
        quantize(nc, eye_c[:, : 2 * P], eye_s[:, : 2 * P], eye_lo[:])
        quantize(nc, eye_c[:, 2 * P :], eye_s[:, 2 * P :], eye_hi[:])

        v_s = sb.tile([P, J], U8, name="v_s", tag="identity", align_bytes=64)
        nc.vector.tensor_copy(v_s[:], tab_s[:].indirect(offsets[:]))

        wq_in = sb.tile([P, N, PACK], BF16, name="wq_in", tag="first_stage", align_bytes=64)
        nc.scalar.copy(out=by_runs_dst(wq_in[:]), in_=by_runs_src(wt_raw[:]))
        wq_c = sb.tile([P, N], U32, name="wq_c", align_bytes=64)
        wq_s = sb.tile([P, N], U8, name="wq_s", align_bytes=64)
        quantize(nc, wq_c[:], wq_s[:], wq_in[:])

        v_c = sb.tile([P, J], U32, name="v_c", tag="first_stage", align_bytes=64)
        nc.vector.tensor_copy(v_c[:], tab_w[:].bitcast(U32).indirect(offsets[:]))

        wr_in = sb.tile([P, N, PACK], BF16, name="wr_in", tag="vector_stage", align_bytes=64)
        for b in range(N_BLOCKS):
            cols = slice(b * P, (b + 1) * P)
            decoded = psum.tile([P, PACK, P], F32, name="decoded%d" % b, tag="bank%d" % (N_BLOCKS + b))
            for t in range(PACK):
                rows = slice(t * P, (t + 1) * P)
                mx(nc, decoded[:, t, :], eye_c[:, rows], eye_s[:, rows], wq_c[:, cols], wq_s[:, cols], True, True)
            nc.vector.tensor_tensor(out=by_runs_dst(wr_in[:, cols, :]), in0=by_runs_src(wt_raw[:, :, cols]),
                                    in1=by_runs_src(decoded[:]), op=mybir.AluOpType.subtract)
        wr_c = sb.tile([P, N], U32, name="wr_c", align_bytes=64)
        wr_s = sb.tile([P, N], U8, name="wr_s", align_bytes=64)
        quantize(nc, wr_c[:], wr_s[:], wr_in[:])

        x_c, x_s = {}, {}
        for a in range(X_PASSES):
            for h in range(J_HALVES):
                x_s[a, h] = sb.tile([P, BANK], U8, name="x_s%d%d" % (a, h), align_bytes=64)

        def interleave(copy, src, tag):
            staged = sb.tile([P, src.shape[2], PACK], BF16, name="staged_" + tag, tag=tag, align_bytes=64)
            copy(out=by_runs_dst(staged[:]), in_=by_runs_src(src))
            return staged

        staged_00 = interleave(nc.scalar.copy, x_raw[0, 0][:], "x_in00")
        staged_01 = interleave(nc.scalar.copy, x_raw[0, 1][:], "x_in01")
        x_c[0, 0] = sb.tile([P, BANK], U32, name="x_c00", tag="vector_stage", align_bytes=64)
        quantize(nc, x_c[0, 0][:], x_s[0, 0][:], staged_00[:])
        x_c[0, 1] = sb.tile([P, BANK], U32, name="x_c01", tag="x_in00", align_bytes=64)
        quantize(nc, x_c[0, 1][:], x_s[0, 1][:], staged_01[:])

        x_c[1, 0] = sb.tile([P, BANK], U32, name="x_c10", align_bytes=64)
        x_c[1, 1] = sb.tile([P, BANK], U32, name="x_c11", align_bytes=64)
        staged_10 = interleave(nc.scalar.copy, x_raw[1, 0][:], "last_stage")
        quantize(nc, x_c[1, 0][:], x_s[1, 0][:], staged_10[:])
        lo, hi = slice(0, BANK // 2), slice(BANK // 2, BANK)
        staged_lo = interleave(nc.vector.tensor_copy, x_raw[1, 1][:, :, lo], "last_stage")
        staged_hi = interleave(nc.scalar.copy, x_raw[1, 1][:, :, hi], "x_in11")
        quantize(nc, x_c[1, 1][:, lo], x_s[1, 1][:, lo], staged_lo[:])
        quantize(nc, x_c[1, 1][:, hi], x_s[1, 1][:, hi], staged_hi[:])

        for b in range(N_BLOCKS):
            cols = slice(b * P, (b + 1) * P)
            res = sb.tile([P, J], F32, name="res%d" % b, align_bytes=64)
            for h in range(J_HALVES):
                toks = slice(h * BANK, (h + 1) * BANK)
                acc = psum.tile([P, BANK], F32, name="acc%d%d" % (b, h), tag="bank%d" % (N_BLOCKS + b if h else b % 2))
                mx(nc, acc[:], wq_c[:, cols], wq_s[:, cols], v_c[:, toks], v_s[:, toks], True, False)
                mx(nc, acc[:], wr_c[:, cols], wr_s[:, cols], v_c[:, toks], v_s[:, toks], False, False)
                for a in reversed(range(X_PASSES)):
                    mx(nc, acc[:], wx_w[b // 2][:, a, (b % 2) * P : (b % 2 + 1) * P], wx_s[:, a, cols], x_c[a, h][:], x_s[a, h][:],
                       False, a == 0)
                y = sb.tile([P, BANK], F32, name="y%d%d" % (b, h), align_bytes=64)
                nc.scalar.copy(out=y[:], in_=acc[:])
                last = (b, h) == (N_BLOCKS - 1, J_HALVES - 1)
                width = BANK // 2 if last else BANK
                for j0 in range(0, BANK, width):
                    part = slice(h * BANK + j0, h * BANK + j0 + width)
                    picked = r_rows[b][:].indirect(offsets[:, part.start // 16 : part.stop // 16])
                    nc.vector.tensor_tensor(res[:, part], picked, y[:, j0 : j0 + width], mybir.AluOpType.add)
                    if b == N_BLOCKS - 1:
                        nc.sync.dma_start(out=out[cols, part], in_=res[:, part])
            if b < N_BLOCKS - 1:
                nc.sync.dma_start(out=out[cols, :], in_=res[:])
